import numpy as np
import ml_dtypes


def mxq(x, axis, fmt="e4m3"):
    dtype, down = {"e4m3": (ml_dtypes.float8_e4m3fn, 7), "e5m2": (ml_dtypes.float8_e5m2, 14)}[fmt]
    v = np.moveaxis(np.asarray(x, np.float32).astype(ml_dtypes.bfloat16).astype(np.float64), axis, -1)
    blocks = v.reshape(v.shape[:-1] + (-1, 32))
    amax = np.abs(blocks).max(-1, keepdims=True)
    byte = np.maximum(np.where(amax > 0, np.frexp(amax)[1] - 1 + 127, 0) - down, 1)
    scale = np.exp2(byte - 127.0)
    codes = (blocks / scale).astype(np.float32).astype(dtype).astype(np.float64)
    return np.moveaxis((codes * scale).reshape(v.shape), -1, axis)


WIDE = False


def mx_kscale(k):
    if not WIDE:
        return np.ones(k)
    levels = np.array([10, -10, 5, -5, 0])
    if k % 512:
        return np.exp2(np.random.permutation(np.resize(levels, k // 32))).repeat(32)
    a = np.empty((k // 512, 16))
    for p in range(k // 512):
        a[p, :8] = np.random.permutation(np.resize(levels, 8))
        for g in range(8):
            far = levels[np.abs(levels - a[p, g]) >= 10]
            a[p, g + 8] = far[np.random.randint(len(far))]
    return np.exp2(a.ravel()).repeat(32)


def f64(x):
    return np.asarray(x).astype(np.float64)


def striped(idx):
    return np.tile(np.asarray(idx).reshape(-1, 16).T, (8, 1)).astype(np.uint16)


def unstriped(offs):
    return offs[:16].T.reshape(-1).astype(np.int64)


E2M1 = np.array([0.0, 0.5, 1.0, 1.5, 2.0, 3.0, 4.0, 6.0, -0.0, -0.5, -1.0, -1.5, -2.0, -3.0, -4.0, -6.0])


def pack_weight(w, fmt):
    k, n = w.shape
    w = f64(np.asarray(w, np.float32).astype(ml_dtypes.bfloat16)).reshape(k // 32, 32, n)
    amax = np.abs(w).max(1)
    if fmt == "e4m3":
        byte = np.frexp(amax)[1] - 1 + 127 - 7
    else:
        mant, ex = np.frexp(amax / 6.0)
        byte = np.where(mant > 0.5, ex, ex - 1) + 127
    byte = np.clip(np.where(amax > 0, byte, 1), 1, 254)
    scaled = (w * np.exp2(127.0 - byte)[:, None, :]).reshape(k, n).astype(np.float32)
    by_word = np.ascontiguousarray(scaled.reshape(k // 512, 128, 4, n).transpose(0, 1, 3, 2))
    if fmt == "e4m3":
        words = by_word.astype(ml_dtypes.float8_e4m3fn).view(np.uint8)
    else:
        c = by_word.astype(ml_dtypes.float4_e2m1fn).view(np.uint8) & 0xF
        words = (c[..., 0::2] | (c[..., 1::2] << 4)).reshape(k // 512, 128, 2 * n)
    return np.ascontiguousarray(words), np.ascontiguousarray(byte.astype(np.uint8).reshape(k // 512, 16, n))


def unpack_weight(words, scales, fmt):
    g, _, n = scales.shape
    words = np.ascontiguousarray(words).reshape(g, 128, n, -1)
    if fmt == "e4m3":
        vals = words.view(ml_dtypes.float8_e4m3fn).astype(np.float64)
    else:
        nib = np.empty((g, 128, n, 4), np.uint8)
        nib[..., 0::2] = words & 0xF
        nib[..., 1::2] = words >> 4
        vals = E2M1[nib]
    vals = vals * np.repeat(np.exp2(scales.astype(np.float64) - 127.0), 8, axis=1)[..., None]
    return vals.transpose(0, 1, 3, 2).reshape(g * 512, n)


D, T, I, Q, J, U, M = 512, 2048, 512, 128, 128, 512, 2048


def setup_inputs():
    n = np.random.standard_normal
    idx = np.random.permutation(T)[:I]
    idx2 = np.random.permutation(U)[:J]
    idx3 = np.random.permutation(M)[:I]
    fd = mx_kscale(D)
    keysp = pack_weight(n((D, T)) / fd[:, None], "e2m1")
    return {
        "query": (n((D, Q)) * 1.2 / np.sqrt(D) * fd[:, None]).astype(np.float32),
        "keys_words": keysp[0],
        "keys_scales": keysp[1],
        "peers": (n((D, U)) * 1.2 / np.sqrt(D) * np.random.uniform(0.3, 1.5, (1, U)) * fd[:, None]).astype(np.float32),
        "kw1": (np.random.uniform(0.2, 2.0, (1, J))).astype(np.float32),
        "lam": (np.random.uniform(1.0, 2.5, (1, Q))).astype(np.float32),
        "gain": (np.random.uniform(0.5, 1.5, (Q, 1))).astype(np.float32),
        "old": (np.random.uniform(0.0, 2.0, (Q, M))).astype(np.float32),
        "fade": (np.random.uniform(0.3, 0.9, (Q, 1))).astype(np.float32),
        "offs": striped(idx),
        "offs2": striped(idx2),
        "offs3": striped(idx3),
    }


def reference(query, keys_words, keys_scales, peers, kw1, lam, gain, old, fade, offs, offs2, offs3):
    idx = unstriped(offs)
    idx2 = unstriped(offs2)
    idx3 = unstriped(offs3)
    keysu = unpack_weight(keys_words, keys_scales, "e2m1")
    keysidxg = keysu[:, idx]
    queryq = mxq(f64(query), 0, "e4m3")
    a0 = keysidxg.T @ queryq
    peersidx2q = mxq(f64(peers)[:, idx2], 0, "e4m3")
    kk = keysidxg.T @ peersidx2q
    m1 = np.mean(np.square(kk) * f64(kw1), axis=1, keepdims=True)
    s0 = a0 / (m1 * f64(lam) + 1.0)
    s = s0.T
    p1 = np.exp(s - np.max(s, axis=1, keepdims=True))
    z1 = np.sum(p1, axis=1, keepdims=True)
    k1 = (1.0 - np.max(p1, axis=1, keepdims=True) / z1) * f64(gain) + 1.0
    s2 = s * k1
    p = np.exp(s2 - np.max(s2, axis=1, keepdims=True))
    w = p / np.sum(p, axis=1, keepdims=True)
    ws = w * 256.0
    wf = np.zeros((Q, M))
    wf[:, idx3] = ws
    y = f64(old) * f64(fade) + wf
    return y

@@ -1,0 +1,193 @@
+from contextlib import ExitStack
+
+import concourse.mybir as mybir
+from concourse.masks import make_identity
+
+D, T, I, Q, J, U, M = 512, 2048, 512, 128, 128, 512, 2048
+FLOPS = 2 * D * I * (Q + J)
+
+F32 = mybir.dt.float32
+BF16 = mybir.dt.bfloat16
+I32 = mybir.dt.int32
+U32 = mybir.dt.uint32
+U16 = mybir.dt.uint16
+U8 = mybir.dt.uint8
+FP8X4 = mybir.dt.float8_e4m3fn_x4
+FP4X4 = mybir.dt.float4_e2m1fn_x4
+ALU = mybir.AluOpType
+ACT = mybir.ActivationFunctionType
+
+P = 128
+PACK = 4
+TILES = I // P
+HALF = I // 2
+CHUNK = 512
+
+
+def tile_attend_crowded_peaked_counts_kernel(tc, query, keys_words, keys_scales, peers, kw1, lam, gain, old, fade, offs, offs2, offs3, out):
+    nc = tc.nc
+    with ExitStack() as ctx:
+        sb = ctx.enter_context(tc.tile_pool(name="sb", bufs=1))
+        ps = ctx.enter_context(tc.psum_pool(name="ps", bufs=1))
+
+        scale_pool = sb.tile([P, T], U8, align_bytes=64)
+        nc.gpsimd.memset(scale_pool[:].bitcast(I32), 0)
+        one = sb.tile([P, 1], F32)
+        nc.gpsimd.memset(one[:], 1.0)
+
+        key_list = sb.tile([P, I // 16], U16)
+        peer_list = sb.tile([P, J // 16], U16)
+        place_list = sb.tile([P, I // 16], U16)
+        nc.sync.dma_start(key_list[:], offs)
+        for quad in range(4):
+            queue = nc.scalar if quad % 2 else nc.sync
+            queue.dma_start(scale_pool[32 * quad : 32 * quad + 4, :].bitcast(I32), keys_scales[0, 4 * quad : 4 * quad + 4, :].bitcast(I32))
+        nc.sync.dma_start(peer_list[:], offs2)
+        warm = sb.tile([P, 1], F32)
+        nc.scalar.activation(warm[:], one[:], ACT.Abs_reciprocal_sqrt)
+        peer_rows = peers.rearrange("(p t) u -> p t u", t=PACK)
+        peer_pool01 = sb.tile([P, 2, U], F32)
+        nc.sync.dma_start(peer_pool01[:], peer_rows[:, 0:2, :])
+        peer_pool2 = sb.tile([P, U], F32)
+        nc.sync.dma_start(peer_pool2[:], peer_rows[:, 2, :])
+        peer_pool3 = sb.tile([P, U], F32)
+        nc.sync.dma_start(peer_pool3[:], peer_rows[:, 3, :])
+        word_pool = sb.tile([P, T], U16, align_bytes=64)
+        nc.sync.dma_start(word_pool[:].bitcast(I32), keys_words[0].bitcast(I32))
+        query_raw = sb.tile([P, PACK, Q], F32)
+        nc.sync.dma_start(query_raw[:], query.rearrange("(p t) q -> p t q", t=PACK))
+        kw_rows = sb.tile([P, J], F32)
+        nc.sync.dma_start(kw_rows[:], kw1[0].partition_broadcast(P))
+        lam_rows = sb.tile([P, Q], F32)
+        nc.sync.dma_start(lam_rows[:], lam[0].partition_broadcast(P))
+        gain_col = sb.tile([P, 1], F32)
+        nc.sync.dma_start(gain_col[:], gain)
+        fade_col = sb.tile([P, 1], F32)
+        nc.sync.dma_start(fade_col[:], fade)
+        nc.sync.dma_start(place_list[:], offs3)
+        old_sb = sb.tile([P, M], F32)
+        nc.sync.dma_start(old_sb[:], old)
+
+        placed = sb.tile([P, M], F32)
+        nc.vector.memset(placed[:], 0.0)
+        ident = sb.tile([P, P], F32)
+        make_identity(nc, ident[:])
+
+        key_scales = sb.tile([P, I], U8, align_bytes=64)
+        nc.vector.tensor_copy(key_scales[:], scale_pool[:].indirect(key_list[:]))
+        peer_bf = sb.tile([P, J, PACK], BF16, align_bytes=64)
+        peer_raw = sb.tile([P, 2, J], F32)
+        for t in range(2):
+            nc.vector.tensor_copy(peer_raw[:, t, :], peer_pool01[:, t, :].indirect(peer_list[:]))
+        nc.scalar.copy(peer_bf[:, :, 0:2], peer_raw[:].rearrange("p t j -> p j t"))
+        nc.vector.tensor_copy(peer_bf[:, :, 2], peer_pool2[:].indirect(peer_list[:]))
+        nc.vector.tensor_copy(peer_bf[:, :, 3], peer_pool3[:].indirect(peer_list[:]))
+        peer_codes = sb.tile([P, J], U32, align_bytes=64)
+        peer_scales = sb.tile([P, J], U8, align_bytes=64)
+        nc.vector.quantize_mx(out=peer_codes[:].bitcast(FP8X4), scales=peer_scales[:], in_=peer_bf[:].rearrange("p j t -> p (j t)"))
+        key_words = []
+        for h in range(2):
+            words = sb.tile([P, HALF], U16, align_bytes=64, name=f"key_words{h}")
+            nc.vector.tensor_copy(words[:], word_pool[:].indirect(key_list[:, 16 * h : 16 * h + 16]))
+            key_words.append(words)
+
+        def keys_times(bank_cols, tile, codes, scales):
+            nc.tensor.matmul_mx(
+                out=bank_cols,
+                lhsT=key_words[tile // 2][:, (tile % 2) * P : (tile % 2 + 1) * P].bitcast(FP4X4),
+                lhsT_scale=key_scales[:, tile * P : (tile + 1) * P],
+                rhs=codes[:].bitcast(FP8X4),
+                rhs_scale=scales[:],
+                start=True,
+                stop=True,
+            )
+
+        query_bf = sb.tile([P, Q, PACK], BF16, align_bytes=64)
+        nc.scalar.copy(query_bf[:], query_raw[:].rearrange("p t q -> p q t"))
+        query_codes = sb.tile([P, Q], U32, align_bytes=64)
+        query_scales = sb.tile([P, Q], U8, align_bytes=64)
+        nc.vector.quantize_mx(out=query_codes[:].bitcast(FP8X4), scales=query_scales[:], in_=query_bf[:].rearrange("p q t -> p (q t)"))
+        squares = sb.tile([P, TILES, J], F32)
+        for h in range(2):
+            kk = ps.tile([P, 2, J], F32, name=f"kk{h}")
+            for c in range(2):
+                keys_times(kk[:, c, :], 2 * h + c, peer_codes, peer_scales)
+            nc.scalar.activation(squares[:, 2 * h : 2 * h + 2, :], kk[:], ACT.Square)
+
+        a0 = []
+        for h in range(2):
+            bank = ps.tile([P, 2, Q], F32, name=f"a0_{h}")
+            for c in range(2):
+                keys_times(bank[:, c, :], 2 * h + c, query_codes, query_scales)
+            a0.append(bank)
+
+        weighted = sb.tile([P, TILES, J], F32)
+        m1 = sb.tile([P, TILES], F32)
+        root = sb.tile([P, TILES, Q], F32)
+        positive = sb.tile([P, TILES, Q], F32)
+        for tile in range(TILES):
+            m1_col = m1[:, tile : tile + 1]
+            nc.vector.scalar_tensor_tensor(weighted[:, tile, :], squares[:, tile, :], 1.0 / J, kw_rows[:], ALU.mult, ALU.mult, accum_out=m1_col)
+            nc.scalar.activation(root[:, tile, :], lam_rows[:], ACT.Abs_reciprocal_sqrt, bias=1.0, scale=m1_col)
+        for tile in range(TILES):
+            nc.vector.tensor_scalar(positive[:, tile, :], lam_rows[:], m1[:, tile : tile + 1], -1.0, ALU.mult, ALU.is_ge)
+
+        inverse = sb.tile([P, TILES, Q], F32)
+        signed = sb.tile([P, TILES, Q], F32)
+        neg_t = sb.tile([P, TILES, Q], F32)
+        neg_s = sb.tile([P, I], F32)
+        low = sb.tile([P, 2], F32)
+        for h in range(2):
+            two = slice(2 * h, 2 * h + 2)
+            nc.scalar.activation(inverse[:, two, :], root[:, two, :], ACT.Square)
+            nc.vector.scalar_tensor_tensor(signed[:, two, :], positive[:, two, :], -0.5, a0[h][:], ALU.add, ALU.mult)
+            nc.vector.scalar_tensor_tensor(neg_t[:, two, :], signed[:, two, :], -2.0, inverse[:, two, :], ALU.mult, ALU.mult)
+            turned = ps.tile([P, HALF], F32, name=f"turned{h}")
+            for c in range(2):
+                nc.tensor.transpose(turned[:, c * P : (c + 1) * P], neg_t[:, 2 * h + c, :], ident[:])
+            nc.vector.tensor_scalar(
+                neg_s[:, h * HALF : (h + 1) * HALF], turned[:], 1.0, low[:, 0:1] if h else None, ALU.mult, ALU.min, accum_out=low[:, h : h + 1]
+            )
+        neg_max = low[:, 1:2]
+
+        gain_plus = sb.tile([P, 1], F32)
+        nc.vector.tensor_scalar(gain_plus[:], gain_col[:], 1.0, None, ALU.add)
+        p1 = sb.tile([P, I], F32)
+        z1 = sb.tile([P, 1], F32)
+        nc.scalar.activation(p1[:], neg_s[:], ACT.Exp, bias=neg_max, scale=-1.0, accum_out=z1[:])
+        below = sb.tile([P, I], F32, tag="below_then_faded")
+        spread = sb.tile([P, 1], F32)
+        nc.vector.tensor_scalar(below[:], neg_s[:], neg_max, None, ALU.subtract, ALU.max, accum_out=spread[:])
+        share = sb.tile([P, 1], F32)
+        nc.vector.reciprocal(share[:], z1[:])
+        neg_spread = sb.tile([P, 1], F32)
+        nc.vector.tensor_scalar(neg_spread[:], spread[:], -1.0, None, ALU.mult)
+        neg_k1 = sb.tile([P, 1], F32)
+        nc.vector.tensor_scalar(neg_k1[:], share[:], gain_col[:], gain_plus[:], ALU.mult, ALU.subtract)
+        shift = sb.tile([P, 1], F32)
+        nc.vector.tensor_scalar(shift[:], neg_spread[:], neg_k1[:], 0.0, ALU.mult, ALU.min)
+
+        p = sb.tile([P, I], F32)
+        z2 = sb.tile([P, 2], F32)
+        for h in range(2):
+            cols = slice(h * HALF, (h + 1) * HALF)
+            nc.scalar.activation(p[:, cols], below[:, cols], ACT.Exp, bias=shift[:], scale=neg_k1[:], accum_out=z2[:, h : h + 1])
+        total = sb.tile([P, 1], F32)
+        nc.scalar.activation(total[:], z2[:, 0:1], ACT.Identity, bias=z2[:, 1:2])
+        total_256 = sb.tile([P, 1], F32)
+        nc.scalar.activation(total_256[:], total[:], ACT.Copy, scale=1.0 / 256.0)
+        factor = sb.tile([P, 1], F32)
+        nc.vector.tensor_copy(placed[:].indirect(place_list[:, 0:16]), p[:, 0:HALF])
+        nc.vector.reciprocal(factor[:], total_256[:])
+        nc.vector.tensor_copy(placed[:].indirect(place_list[:, 16:32]), p[:, HALF:I])
+
+        faded = sb.tile([P, M], F32, tag="below_then_faded")
+        result = sb.tile([P, M], F32)
+        for c in range(M // CHUNK):
+            cols = slice(c * CHUNK, (c + 1) * CHUNK)
+            nc.scalar.activation(faded[:, cols], old_sb[:, cols], ACT.Copy, scale=fade_col[:])
+        edges = (0, 256, 768, 1280, 1792, M)
+        for c in range(len(edges) - 1):
+            cols = slice(edges[c], edges[c + 1])
+            nc.vector.scalar_tensor_tensor(result[:, cols], placed[:, cols], factor[:], faded[:, cols], ALU.mult, ALU.add)
+            nc.sync.dma_start(out[:, cols], result[:, cols])

@@ -31,35 +31,39 @@ def tile_attend_crowded_peaked_counts_kernel(tc, query, keys_words, keys_scales,
         ps = ctx.enter_context(tc.psum_pool(name="ps", bufs=1))
 
         scale_pool = sb.tile([P, T], U8, align_bytes=64)
-        nc.gpsimd.memset(scale_pool[:].bitcast(I32), 0)
+        nc.vector.memset(scale_pool[:].bitcast(I32), 0)
+        ident = sb.tile([P, P], F32)
+        nc.vector.memset(ident[:], 0.0)
+        make_identity(nc, ident[:], nomemset=True)
         one = sb.tile([P, 1], F32)
-        nc.gpsimd.memset(one[:], 1.0)
+        nc.vector.memset(one[:], 1.0)
 
         key_list = sb.tile([P, I // 16], U16)
         peer_list = sb.tile([P, J // 16], U16)
         place_list = sb.tile([P, I // 16], U16)
+        peer_rows = peers.rearrange("(p t) u -> p t u", t=PACK)
+        peer_pool0 = sb.tile([P, U], F32)
+        peer_pool1 = sb.tile([P, U], F32)
+        peer_pool23 = sb.tile([P, 2, U], F32)
+        nc.sync.dma_start(peer_list[:], offs2)
+        nc.sync.dma_start(peer_pool0[:], peer_rows[:, 0, :])
         nc.sync.dma_start(key_list[:], offs)
         for quad in range(4):
-            queue = nc.scalar if quad % 2 else nc.sync
-            queue.dma_start(scale_pool[32 * quad : 32 * quad + 4, :].bitcast(I32), keys_scales[0, 4 * quad : 4 * quad + 4, :].bitcast(I32))
-        nc.sync.dma_start(peer_list[:], offs2)
+            nc.sync.dma_start(scale_pool[32 * quad : 32 * quad + 4, :].bitcast(I32), keys_scales[0, 4 * quad : 4 * quad + 4, :].bitcast(I32))
+        nc.sync.dma_start(peer_pool1[:], peer_rows[:, 1, :])
+        nc.sync.dma_start(peer_pool23[:], peer_rows[:, 2:4, :])
+        kw_col = sb.tile([P, 1], F32)
+        lam_col = sb.tile([P, 1], F32)
+        with nc.allow_non_contiguous_dma(reason="one value to a partition"):
+            nc.gpsimd.dma_start(lam_col[:], lam.rearrange("o q -> q o"))
         warm = sb.tile([P, 1], F32)
         nc.scalar.activation(warm[:], one[:], ACT.Abs_reciprocal_sqrt)
-        peer_rows = peers.rearrange("(p t) u -> p t u", t=PACK)
-        peer_pool01 = sb.tile([P, 2, U], F32)
-        nc.sync.dma_start(peer_pool01[:], peer_rows[:, 0:2, :])
-        peer_pool2 = sb.tile([P, U], F32)
-        nc.sync.dma_start(peer_pool2[:], peer_rows[:, 2, :])
-        peer_pool3 = sb.tile([P, U], F32)
-        nc.sync.dma_start(peer_pool3[:], peer_rows[:, 3, :])
         word_pool = sb.tile([P, T], U16, align_bytes=64)
         nc.sync.dma_start(word_pool[:].bitcast(I32), keys_words[0].bitcast(I32))
         query_raw = sb.tile([P, PACK, Q], F32)
         nc.sync.dma_start(query_raw[:], query.rearrange("(p t) q -> p t q", t=PACK))
-        kw_rows = sb.tile([P, J], F32)
-        nc.sync.dma_start(kw_rows[:], kw1[0].partition_broadcast(P))
-        lam_rows = sb.tile([P, Q], F32)
-        nc.sync.dma_start(lam_rows[:], lam[0].partition_broadcast(P))
+        with nc.allow_non_contiguous_dma(reason="one value to a partition"):
+            nc.sync.dma_start(kw_col[:], kw1.rearrange("o j -> j o"))
         gain_col = sb.tile([P, 1], F32)
         nc.sync.dma_start(gain_col[:], gain)
         fade_col = sb.tile([P, 1], F32)
@@ -70,18 +74,25 @@ def tile_attend_crowded_peaked_counts_kernel(tc, query, keys_words, keys_scales,
 
         placed = sb.tile([P, M], F32)
         nc.vector.memset(placed[:], 0.0)
-        ident = sb.tile([P, P], F32)
-        make_identity(nc, ident[:])
 
+        lam_bank = ps.tile([P, Q], F32)
+        nc.tensor.transpose(lam_bank[:], lam_col[:].to_broadcast([P, P]), ident[:])
+        lam_sb = sb.tile([P, Q], F32)
+        nc.scalar.copy(lam_sb[:], lam_bank[:])
+        lam_rows = lam_sb[:]
+        kw_bank = ps.tile([P, J], F32)
+        nc.tensor.transpose(kw_bank[:], kw_col[:].to_broadcast([P, P]), ident[:])
+        kw_rows = kw_bank[:]
+
+        peer_raw = sb.tile([P, 2, J], F32)
+        nc.vector.tensor_copy(peer_raw[:, 0, :], peer_pool0[:].indirect(peer_list[:]))
+        nc.vector.tensor_copy(peer_raw[:, 1, :], peer_pool1[:].indirect(peer_list[:]))
         key_scales = sb.tile([P, I], U8, align_bytes=64)
         nc.vector.tensor_copy(key_scales[:], scale_pool[:].indirect(key_list[:]))
         peer_bf = sb.tile([P, J, PACK], BF16, align_bytes=64)
-        peer_raw = sb.tile([P, 2, J], F32)
-        for t in range(2):
-            nc.vector.tensor_copy(peer_raw[:, t, :], peer_pool01[:, t, :].indirect(peer_list[:]))
         nc.scalar.copy(peer_bf[:, :, 0:2], peer_raw[:].rearrange("p t j -> p j t"))
-        nc.vector.tensor_copy(peer_bf[:, :, 2], peer_pool2[:].indirect(peer_list[:]))
-        nc.vector.tensor_copy(peer_bf[:, :, 3], peer_pool3[:].indirect(peer_list[:]))
+        nc.vector.tensor_copy(peer_bf[:, :, 2], peer_pool23[:, 0, :].indirect(peer_list[:]))
+        nc.vector.tensor_copy(peer_bf[:, :, 3], peer_pool23[:, 1, :].indirect(peer_list[:]))
         peer_codes = sb.tile([P, J], U32, align_bytes=64)
         peer_scales = sb.tile([P, J], U8, align_bytes=64)
         nc.vector.quantize_mx(out=peer_codes[:].bitcast(FP8X4), scales=peer_scales[:], in_=peer_bf[:].rearrange("p j t -> p (j t)"))
@@ -103,23 +114,20 @@ def tile_attend_crowded_peaked_counts_kernel(tc, query, keys_words, keys_scales,
             )
 
         query_bf = sb.tile([P, Q, PACK], BF16, align_bytes=64)
-        nc.scalar.copy(query_bf[:], query_raw[:].rearrange("p t q -> p q t"))
+        nc.vector.tensor_copy(query_bf[:], query_raw[:].rearrange("p t q -> p q t"))
         query_codes = sb.tile([P, Q], U32, align_bytes=64)
         query_scales = sb.tile([P, Q], U8, align_bytes=64)
         nc.vector.quantize_mx(out=query_codes[:].bitcast(FP8X4), scales=query_scales[:], in_=query_bf[:].rearrange("p q t -> p (q t)"))
         squares = sb.tile([P, TILES, J], F32)
-        for h in range(2):
-            kk = ps.tile([P, 2, J], F32, name=f"kk{h}")
-            for c in range(2):
-                keys_times(kk[:, c, :], 2 * h + c, peer_codes, peer_scales)
-            nc.scalar.activation(squares[:, 2 * h : 2 * h + 2, :], kk[:], ACT.Square)
+        for first, count in ((0, 1), (1, 1), (2, 2)):
+            kk = ps.tile([P, count, J], F32, name=f"kk{first}")
+            for c in range(count):
+                keys_times(kk[:, c, :], first + c, peer_codes, peer_scales)
+            nc.scalar.activation(squares[:, first : first + count, :], kk[:], ACT.Square)
 
-        a0 = []
-        for h in range(2):
-            bank = ps.tile([P, 2, Q], F32, name=f"a0_{h}")
-            for c in range(2):
-                keys_times(bank[:, c, :], 2 * h + c, query_codes, query_scales)
-            a0.append(bank)
+        a0 = ps.tile([P, TILES, Q], F32)
+        for tile in range(TILES):
+            keys_times(a0[:, tile, :], tile, query_codes, query_scales)
 
         weighted = sb.tile([P, TILES, J], F32)
         m1 = sb.tile([P, TILES], F32)
@@ -127,26 +135,30 @@ def tile_attend_crowded_peaked_counts_kernel(tc, query, keys_words, keys_scales,
         positive = sb.tile([P, TILES, Q], F32)
         for tile in range(TILES):
             m1_col = m1[:, tile : tile + 1]
-            nc.vector.scalar_tensor_tensor(weighted[:, tile, :], squares[:, tile, :], 1.0 / J, kw_rows[:], ALU.mult, ALU.mult, accum_out=m1_col)
-            nc.scalar.activation(root[:, tile, :], lam_rows[:], ACT.Abs_reciprocal_sqrt, bias=1.0, scale=m1_col)
+            nc.vector.scalar_tensor_tensor(weighted[:, tile, :], squares[:, tile, :], 1.0 / J, kw_rows, ALU.mult, ALU.mult, accum_out=m1_col)
+            nc.scalar.activation(root[:, tile, :], lam_rows, ACT.Abs_reciprocal_sqrt, bias=1.0, scale=m1_col)
         for tile in range(TILES):
-            nc.vector.tensor_scalar(positive[:, tile, :], lam_rows[:], m1[:, tile : tile + 1], -1.0, ALU.mult, ALU.is_ge)
+            nc.vector.tensor_scalar(positive[:, tile, :], lam_rows, m1[:, tile : tile + 1], -1.0, ALU.mult, ALU.is_ge)
 
         inverse = sb.tile([P, TILES, Q], F32)
         signed = sb.tile([P, TILES, Q], F32)
         neg_t = sb.tile([P, TILES, Q], F32)
         neg_s = sb.tile([P, I], F32)
         low = sb.tile([P, 2], F32)
-        for h in range(2):
-            two = slice(2 * h, 2 * h + 2)
+        halves = (slice(0, 2), slice(2, 4))
+        for h, two in enumerate(halves):
             nc.scalar.activation(inverse[:, two, :], root[:, two, :], ACT.Square)
-            nc.vector.scalar_tensor_tensor(signed[:, two, :], positive[:, two, :], -0.5, a0[h][:], ALU.add, ALU.mult)
+            nc.vector.scalar_tensor_tensor(signed[:, two, :], positive[:, two, :], -0.5, a0[:, two, :], ALU.add, ALU.mult)
+        turned = []
+        for h, two in enumerate(halves):
             nc.vector.scalar_tensor_tensor(neg_t[:, two, :], signed[:, two, :], -2.0, inverse[:, two, :], ALU.mult, ALU.mult)
-            turned = ps.tile([P, HALF], F32, name=f"turned{h}")
+            bank = ps.tile([P, HALF], F32, name=f"turned{h}")
             for c in range(2):
-                nc.tensor.transpose(turned[:, c * P : (c + 1) * P], neg_t[:, 2 * h + c, :], ident[:])
+                nc.tensor.transpose(bank[:, c * P : (c + 1) * P], neg_t[:, 2 * h + c, :], ident[:])
+            turned.append(bank)
+        for h in range(2):
             nc.vector.tensor_scalar(
-                neg_s[:, h * HALF : (h + 1) * HALF], turned[:], 1.0, low[:, 0:1] if h else None, ALU.mult, ALU.min, accum_out=low[:, h : h + 1]
+                neg_s[:, h * HALF : (h + 1) * HALF], turned[h][:], 1.0, low[:, 0:1] if h else None, ALU.mult, ALU.min, accum_out=low[:, h : h + 1]
             )
         neg_max = low[:, 1:2]
 

from contextlib import ExitStack

import concourse.mybir as mybir
from concourse.masks import make_identity

D, T, I, Q, J, U, M = 512, 2048, 512, 128, 128, 512, 2048
FLOPS = 2 * D * I * (Q + J)

F32 = mybir.dt.float32
BF16 = mybir.dt.bfloat16
I32 = mybir.dt.int32
U32 = mybir.dt.uint32
U16 = mybir.dt.uint16
U8 = mybir.dt.uint8
FP8X4 = mybir.dt.float8_e4m3fn_x4
FP4X4 = mybir.dt.float4_e2m1fn_x4
ALU = mybir.AluOpType
ACT = mybir.ActivationFunctionType

P = 128
PACK = 4
TILES = I // P
HALF = I // 2
CHUNK = 512


def tile_attend_crowded_peaked_counts_kernel(tc, query, keys_words, keys_scales, peers, kw1, lam, gain, old, fade, offs, offs2, offs3, out):
    nc = tc.nc
    with ExitStack() as ctx:
        sb = ctx.enter_context(tc.tile_pool(name="sb", bufs=1))
        ps = ctx.enter_context(tc.psum_pool(name="ps", bufs=1))

        scale_pool = sb.tile([P, T], U8, align_bytes=64)
        nc.vector.memset(scale_pool[:].bitcast(I32), 0)
        ident = sb.tile([P, P], F32)
        nc.vector.memset(ident[:], 0.0)
        make_identity(nc, ident[:], nomemset=True)
        one = sb.tile([P, 1], F32)
        nc.vector.memset(one[:], 1.0)

        key_list = sb.tile([P, I // 16], U16)
        peer_list = sb.tile([P, J // 16], U16)
        place_list = sb.tile([P, I // 16], U16)
        peer_rows = peers.rearrange("(p t) u -> p t u", t=PACK)
        peer_pool0 = sb.tile([P, U], F32)
        peer_pool1 = sb.tile([P, U], F32)
        peer_pool23 = sb.tile([P, 2, U], F32)
        nc.sync.dma_start(peer_list[:], offs2)
        nc.sync.dma_start(peer_pool0[:], peer_rows[:, 0, :])
        nc.sync.dma_start(key_list[:], offs)
        for quad in range(4):
            nc.sync.dma_start(scale_pool[32 * quad : 32 * quad + 4, :].bitcast(I32), keys_scales[0, 4 * quad : 4 * quad + 4, :].bitcast(I32))
        nc.sync.dma_start(peer_pool1[:], peer_rows[:, 1, :])
        nc.sync.dma_start(peer_pool23[:], peer_rows[:, 2:4, :])
        kw_col = sb.tile([P, 1], F32)
        lam_col = sb.tile([P, 1], F32)
        with nc.allow_non_contiguous_dma(reason="one value to a partition"):
            nc.gpsimd.dma_start(lam_col[:], lam.rearrange("o q -> q o"))
        warm = sb.tile([P, 1], F32)
        nc.scalar.activation(warm[:], one[:], ACT.Abs_reciprocal_sqrt)
        word_pool = sb.tile([P, T], U16, align_bytes=64)
        nc.sync.dma_start(word_pool[:].bitcast(I32), keys_words[0].bitcast(I32))
        query_raw = sb.tile([P, PACK, Q], F32)
        nc.sync.dma_start(query_raw[:], query.rearrange("(p t) q -> p t q", t=PACK))
        with nc.allow_non_contiguous_dma(reason="one value to a partition"):
            nc.sync.dma_start(kw_col[:], kw1.rearrange("o j -> j o"))
        gain_col = sb.tile([P, 1], F32)
        nc.sync.dma_start(gain_col[:], gain)
        fade_col = sb.tile([P, 1], F32)
        nc.sync.dma_start(fade_col[:], fade)
        nc.sync.dma_start(place_list[:], offs3)
        old_sb = sb.tile([P, M], F32)
        nc.sync.dma_start(old_sb[:], old)

        placed = sb.tile([P, M], F32)
        nc.vector.memset(placed[:], 0.0)

        lam_bank = ps.tile([P, Q], F32)
        nc.tensor.transpose(lam_bank[:], lam_col[:].to_broadcast([P, P]), ident[:])
        lam_sb = sb.tile([P, Q], F32)
        nc.scalar.copy(lam_sb[:], lam_bank[:])
        lam_rows = lam_sb[:]
        kw_bank = ps.tile([P, J], F32)
        nc.tensor.transpose(kw_bank[:], kw_col[:].to_broadcast([P, P]), ident[:])
        kw_rows = kw_bank[:]

        peer_raw = sb.tile([P, 2, J], F32)
        nc.vector.tensor_copy(peer_raw[:, 0, :], peer_pool0[:].indirect(peer_list[:]))
        nc.vector.tensor_copy(peer_raw[:, 1, :], peer_pool1[:].indirect(peer_list[:]))
        key_scales = sb.tile([P, I], U8, align_bytes=64)
        nc.vector.tensor_copy(key_scales[:], scale_pool[:].indirect(key_list[:]))
        peer_bf = sb.tile([P, J, PACK], BF16, align_bytes=64)
        nc.scalar.copy(peer_bf[:, :, 0:2], peer_raw[:].rearrange("p t j -> p j t"))
        nc.vector.tensor_copy(peer_bf[:, :, 2], peer_pool23[:, 0, :].indirect(peer_list[:]))
        nc.vector.tensor_copy(peer_bf[:, :, 3], peer_pool23[:, 1, :].indirect(peer_list[:]))
        peer_codes = sb.tile([P, J], U32, align_bytes=64)
        peer_scales = sb.tile([P, J], U8, align_bytes=64)
        nc.vector.quantize_mx(out=peer_codes[:].bitcast(FP8X4), scales=peer_scales[:], in_=peer_bf[:].rearrange("p j t -> p (j t)"))
        key_words = []
        for h in range(2):
            words = sb.tile([P, HALF], U16, align_bytes=64, name=f"key_words{h}")
            nc.vector.tensor_copy(words[:], word_pool[:].indirect(key_list[:, 16 * h : 16 * h + 16]))
            key_words.append(words)

        def keys_times(bank_cols, tile, codes, scales):
            nc.tensor.matmul_mx(
                out=bank_cols,
                lhsT=key_words[tile // 2][:, (tile % 2) * P : (tile % 2 + 1) * P].bitcast(FP4X4),
                lhsT_scale=key_scales[:, tile * P : (tile + 1) * P],
                rhs=codes[:].bitcast(FP8X4),
                rhs_scale=scales[:],
                start=True,
                stop=True,
            )

        query_bf = sb.tile([P, Q, PACK], BF16, align_bytes=64)
        nc.vector.tensor_copy(query_bf[:], query_raw[:].rearrange("p t q -> p q t"))
        query_codes = sb.tile([P, Q], U32, align_bytes=64)
        query_scales = sb.tile([P, Q], U8, align_bytes=64)
        nc.vector.quantize_mx(out=query_codes[:].bitcast(FP8X4), scales=query_scales[:], in_=query_bf[:].rearrange("p q t -> p (q t)"))
        squares = sb.tile([P, TILES, J], F32)
        for first, count in ((0, 1), (1, 1), (2, 2)):
            kk = ps.tile([P, count, J], F32, name=f"kk{first}")
            for c in range(count):
                keys_times(kk[:, c, :], first + c, peer_codes, peer_scales)
            nc.scalar.activation(squares[:, first : first + count, :], kk[:], ACT.Square)

        a0 = ps.tile([P, TILES, Q], F32)
        for tile in range(TILES):
            keys_times(a0[:, tile, :], tile, query_codes, query_scales)

        weighted = sb.tile([P, TILES, J], F32)
        m1 = sb.tile([P, TILES], F32)
        root = sb.tile([P, TILES, Q], F32)
        positive = sb.tile([P, TILES, Q], F32)
        for tile in range(TILES):
            m1_col = m1[:, tile : tile + 1]
            nc.vector.scalar_tensor_tensor(weighted[:, tile, :], squares[:, tile, :], 1.0 / J, kw_rows, ALU.mult, ALU.mult, accum_out=m1_col)
            nc.scalar.activation(root[:, tile, :], lam_rows, ACT.Abs_reciprocal_sqrt, bias=1.0, scale=m1_col)
        for tile in range(TILES):
            nc.vector.tensor_scalar(positive[:, tile, :], lam_rows, m1[:, tile : tile + 1], -1.0, ALU.mult, ALU.is_ge)

        inverse = sb.tile([P, TILES, Q], F32)
        signed = sb.tile([P, TILES, Q], F32)
        neg_t = sb.tile([P, TILES, Q], F32)
        neg_s = sb.tile([P, I], F32)
        low = sb.tile([P, 2], F32)
        halves = (slice(0, 2), slice(2, 4))
        for h, two in enumerate(halves):
            nc.scalar.activation(inverse[:, two, :], root[:, two, :], ACT.Square)
            nc.vector.scalar_tensor_tensor(signed[:, two, :], positive[:, two, :], -0.5, a0[:, two, :], ALU.add, ALU.mult)
        turned = []
        for h, two in enumerate(halves):
            nc.vector.scalar_tensor_tensor(neg_t[:, two, :], signed[:, two, :], -2.0, inverse[:, two, :], ALU.mult, ALU.mult)
            bank = ps.tile([P, HALF], F32, name=f"turned{h}")
            for c in range(2):
                nc.tensor.transpose(bank[:, c * P : (c + 1) * P], neg_t[:, 2 * h + c, :], ident[:])
            turned.append(bank)
        for h in range(2):
            nc.vector.tensor_scalar(
                neg_s[:, h * HALF : (h + 1) * HALF], turned[h][:], 1.0, low[:, 0:1] if h else None, ALU.mult, ALU.min, accum_out=low[:, h : h + 1]
            )
        neg_max = low[:, 1:2]

        gain_plus = sb.tile([P, 1], F32)
        nc.vector.tensor_scalar(gain_plus[:], gain_col[:], 1.0, None, ALU.add)
        p1 = sb.tile([P, I], F32)
        z1 = sb.tile([P, 1], F32)
        nc.scalar.activation(p1[:], neg_s[:], ACT.Exp, bias=neg_max, scale=-1.0, accum_out=z1[:])
        below = sb.tile([P, I], F32, tag="below_then_faded")
        spread = sb.tile([P, 1], F32)
        nc.vector.tensor_scalar(below[:], neg_s[:], neg_max, None, ALU.subtract, ALU.max, accum_out=spread[:])
        share = sb.tile([P, 1], F32)
        nc.vector.reciprocal(share[:], z1[:])
        neg_spread = sb.tile([P, 1], F32)
        nc.vector.tensor_scalar(neg_spread[:], spread[:], -1.0, None, ALU.mult)
        neg_k1 = sb.tile([P, 1], F32)
        nc.vector.tensor_scalar(neg_k1[:], share[:], gain_col[:], gain_plus[:], ALU.mult, ALU.subtract)
        shift = sb.tile([P, 1], F32)
        nc.vector.tensor_scalar(shift[:], neg_spread[:], neg_k1[:], 0.0, ALU.mult, ALU.min)

        p = sb.tile([P, I], F32)
        z2 = sb.tile([P, 2], F32)
        for h in range(2):
            cols = slice(h * HALF, (h + 1) * HALF)
            nc.scalar.activation(p[:, cols], below[:, cols], ACT.Exp, bias=shift[:], scale=neg_k1[:], accum_out=z2[:, h : h + 1])
        total = sb.tile([P, 1], F32)
        nc.scalar.activation(total[:], z2[:, 0:1], ACT.Identity, bias=z2[:, 1:2])
        total_256 = sb.tile([P, 1], F32)
        nc.scalar.activation(total_256[:], total[:], ACT.Copy, scale=1.0 / 256.0)
        factor = sb.tile([P, 1], F32)
        nc.vector.tensor_copy(placed[:].indirect(place_list[:, 0:16]), p[:, 0:HALF])
        nc.vector.reciprocal(factor[:], total_256[:])
        nc.vector.tensor_copy(placed[:].indirect(place_list[:, 16:32]), p[:, HALF:I])

        faded = sb.tile([P, M], F32, tag="below_then_faded")
        result = sb.tile([P, M], F32)
        for c in range(M // CHUNK):
            cols = slice(c * CHUNK, (c + 1) * CHUNK)
            nc.scalar.activation(faded[:, cols], old_sb[:, cols], ACT.Copy, scale=fade_col[:])
        edges = (0, 256, 768, 1280, 1792, M)
        for c in range(len(edges) - 1):
            cols = slice(edges[c], edges[c + 1])
            nc.vector.scalar_tensor_tensor(result[:, cols], placed[:, cols], factor[:], faded[:, cols], ALU.mult, ALU.add)
            nc.sync.dma_start(out[:, cols], result[:, cols])
